import numpy as np
import ml_dtypes


def mxq(x, axis, fmt="e4m3"):
    dtype, down = {"e4m3": (ml_dtypes.float8_e4m3fn, 7), "e5m2": (ml_dtypes.float8_e5m2, 14)}[fmt]
    v = np.moveaxis(np.asarray(x, np.float32).astype(ml_dtypes.bfloat16).astype(np.float64), axis, -1)
    blocks = v.reshape(v.shape[:-1] + (-1, 32))
    amax = np.abs(blocks).max(-1, keepdims=True)
    byte = np.maximum(np.where(amax > 0, np.frexp(amax)[1] - 1 + 127, 0) - down, 1)
    scale = np.exp2(byte - 127.0)
    codes = (blocks / scale).astype(np.float32).astype(dtype).astype(np.float64)
    return np.moveaxis((codes * scale).reshape(v.shape), -1, axis)


WIDE = False


def mx_kscale(k):
    if not WIDE:
        return np.ones(k)
    levels = np.array([10, -10, 5, -5, 0])
    if k % 512:
        return np.exp2(np.random.permutation(np.resize(levels, k // 32))).repeat(32)
    a = np.empty((k // 512, 16))
    for p in range(k // 512):
        a[p, :8] = np.random.permutation(np.resize(levels, 8))
        for g in range(8):
            far = levels[np.abs(levels - a[p, g]) >= 10]
            a[p, g + 8] = far[np.random.randint(len(far))]
    return np.exp2(a.ravel()).repeat(32)


def f64(x):
    return np.asarray(x).astype(np.float64)


E2M1 = np.array([0.0, 0.5, 1.0, 1.5, 2.0, 3.0, 4.0, 6.0, -0.0, -0.5, -1.0, -1.5, -2.0, -3.0, -4.0, -6.0])


def pack_weight(w, fmt):
    k, n = w.shape
    w = f64(np.asarray(w, np.float32).astype(ml_dtypes.bfloat16)).reshape(k // 32, 32, n)
    amax = np.abs(w).max(1)
    if fmt == "e4m3":
        byte = np.frexp(amax)[1] - 1 + 127 - 7
    else:
        mant, ex = np.frexp(amax / 6.0)
        byte = np.where(mant > 0.5, ex, ex - 1) + 127
    byte = np.clip(np.where(amax > 0, byte, 1), 1, 254)
    scaled = (w * np.exp2(127.0 - byte)[:, None, :]).reshape(k, n).astype(np.float32)
    by_word = np.ascontiguousarray(scaled.reshape(k // 512, 128, 4, n).transpose(0, 1, 3, 2))
    if fmt == "e4m3":
        words = by_word.astype(ml_dtypes.float8_e4m3fn).view(np.uint8)
    else:
        c = by_word.astype(ml_dtypes.float4_e2m1fn).view(np.uint8) & 0xF
        words = (c[..., 0::2] | (c[..., 1::2] << 4)).reshape(k // 512, 128, 2 * n)
    return np.ascontiguousarray(words), np.ascontiguousarray(byte.astype(np.uint8).reshape(k // 512, 16, n))


def unpack_weight(words, scales, fmt):
    g, _, n = scales.shape
    words = np.ascontiguousarray(words).reshape(g, 128, n, -1)
    if fmt == "e4m3":
        vals = words.view(ml_dtypes.float8_e4m3fn).astype(np.float64)
    else:
        nib = np.empty((g, 128, n, 4), np.uint8)
        nib[..., 0::2] = words & 0xF
        nib[..., 1::2] = words >> 4
        vals = E2M1[nib]
    vals = vals * np.repeat(np.exp2(scales.astype(np.float64) - 127.0), 8, axis=1)[..., None]
    return vals.transpose(0, 1, 3, 2).reshape(g * 512, n)


O, K, R, M, T = 1024, 2048, 512, 1024, 1024


def setup_inputs():
    n = np.random.standard_normal
    s = mx_kscale(K)[:, None]
    u = mx_kscale(R)[:, None]
    x = n((K, T)); x[:O] *= 6.0
    w = n((K, M)) / np.sqrt(K) / s; w[:O] /= 2.0
    p_w8 = pack_weight(w[:O], "e4m3")
    p_w4 = pack_weight(w[O:], "e2m1")
    p_up = pack_weight(n((R, M)) / np.sqrt(R) / u, "e2m1")
    return {
        "x": (x * s).astype(np.float32),
        "w8_words": p_w8[0],
        "w8_scales": p_w8[1],
        "w4_words": p_w4[0],
        "w4_scales": p_w4[1],
        "down": (0.3 * n((K, R)) / np.sqrt(K) / s * u.T).astype(np.float32),
        "up_words": p_up[0],
        "up_scales": p_up[1],
        "prev": (n((1024, 1024))).astype(np.float32),
    }


def reference(x, w8_words, w8_scales, w4_words, w4_scales, down, up_words, up_scales, prev):
    x_ = mxq(f64(x), 0, "e4m3")
    w8_ = unpack_weight(w8_words, w8_scales, "e4m3")
    w4_ = unpack_weight(w4_words, w4_scales, "e2m1")
    down_ = mxq(f64(down), 0, "e4m3")
    up_ = unpack_weight(up_words, up_scales, "e2m1")
    h_ = mxq(down_.T @ x_, 0, "e4m3")
    y = x_[:O].T @ w8_ + x_[O:].T @ w4_ + h_.T @ up_
    return f64(prev) + y

@@ -1,0 +1,359 @@
+from contextlib import ExitStack
+
+import concourse.mybir as mybir
+
+O, K, R, M, T = 1024, 2048, 512, 1024, 1024
+FLOPS = 2 * T * (K * R + K * M + R * M)
+BYTES = 4 * (K * T + K * R + 2 * T * M) + O * M + (K - O) * M // 2 + R * M // 2 + (K + R) * M // 32
+
+F32 = mybir.dt.float32
+BF16 = mybir.dt.bfloat16
+U32 = mybir.dt.uint32
+I32 = mybir.dt.int32
+U8 = mybir.dt.uint8
+FP8X4 = mybir.dt.float8_e4m3fn_x4
+FP4X4 = mybir.dt.float4_e2m1fn_x4
+ADD = mybir.AluOpType.add
+
+P = 128
+PACK = 4
+K_PASS = P * PACK
+N_TILE = 512
+GROUPS = K // K_PASS
+SLICES = ((0, 256), (256, 256), (512, 512))
+W_MAX = 512
+
+
+def tile_mix_three_tm_res_kernel(
+    tc, x, w8_words, w8_scales, w4_words, w4_scales, down, up_words, up_scales, prev, out
+):
+    nc = tc.nc
+    with ExitStack() as ctx:
+        keep = ctx.enter_context(tc.tile_pool(name="keep", bufs=1))
+        xraw = ctx.enter_context(tc.tile_pool(name="xraw", bufs=1))
+        draw = ctx.enter_context(tc.tile_pool(name="draw", bufs=4))
+        group = ctx.enter_context(tc.tile_pool(name="group", bufs=3))
+        hsb = ctx.enter_context(tc.tile_pool(name="hsb", bufs=1))
+        psum = ctx.enter_context(tc.psum_pool(name="psum", bufs=1))
+        ctx.enter_context(tc.manual_schedule())
+
+        w8 = keep.tile([P, 2, M], U32, name="w8", align_bytes=64)
+        w4 = keep.tile([P, 2, 2 * M], U8, name="w4", align_bytes=64)
+        up = keep.tile([P, 2 * M], U8, name="up", align_bytes=64)
+        sc = keep.tile([P, 5, M], U8, name="sc", align_bytes=64)
+        xq, xs, xr = {}, {}, {}
+        dq, ds, dr = {}, {}, {}
+        for s, (t0, w) in enumerate(SLICES):
+            for g in range(GROUPS):
+                xq[s, g] = keep.tile([P, w], U32, name=f"xq{s}{g}", align_bytes=64)
+                xs[s, g] = keep.tile([P, w], U8, name=f"xs{s}{g}", align_bytes=64)
+        for g in range(GROUPS):
+            dq[g] = keep.tile([P, R], U32, name=f"dq{g}", align_bytes=64)
+            ds[g] = keep.tile([P, R], U8, name=f"ds{g}", align_bytes=64)
+        pv = [keep.tile([P, 2, M], F32, name=f"pv{b}") for b in range(4)]
+
+        def load_x(s, g):
+            t0, w = SLICES[s]
+            xr[s, g] = xraw.tile([P, PACK, w], F32, name=f"xr{s}{g}")
+            rows = x[g * K_PASS : (g + 1) * K_PASS, t0 : t0 + w]
+            nc.sync.dma_start(out=xr[s, g][:], in_=rows.rearrange("(p j) w -> p j w", j=PACK))
+
+        def load_d(g):
+            dr[g] = draw.tile([P, PACK, R], F32, name="dr")
+            rows = down[g * K_PASS : (g + 1) * K_PASS, :]
+            nc.sync.dma_start(out=dr[g][:], in_=rows.rearrange("(p j) r -> p j r", j=PACK))
+
+        def load_w8(a):
+            nc.sync.dma_start(
+                out=w8[:, a, :].bitcast(I32), in_=w8_words[a].rearrange("p n i -> p (n i)").bitcast(I32)
+            )
+
+        def load_w4():
+            nc.sync.dma_start(out=w4[:].bitcast(I32), in_=w4_words.rearrange("a p n -> p a n").bitcast(I32))
+
+        def load_up():
+            nc.sync.dma_start(out=up[:].bitcast(I32), in_=up_words[0].bitcast(I32))
+
+        def load_scales(which):
+            for q in range(4):
+                rows = slice(32 * q, 32 * q + 4)
+                src = slice(4 * q, 4 * q + 4)
+                if which == 2:
+                    nc.sync.dma_start(out=sc[rows, 4, :].bitcast(I32), in_=up_scales[0, src, :].bitcast(I32))
+                else:
+                    scales = (w8_scales, w4_scales)[which]
+                    nc.sync.dma_start(
+                        out=sc[rows, 2 * which : 2 * which + 2, :].bitcast(I32),
+                        in_=scales[:, src, :].rearrange("a r n -> r a n").bitcast(I32),
+                    )
+
+        def load_prev(b):
+            rows = prev[b * 256 : (b + 1) * 256, :]
+            nc.sync.dma_start(out=pv[b][:], in_=rows.rearrange("(a p) n -> p a n", p=P))
+
+        def store(t):
+            nc.sync.dma_start(out=out[t * P : (t + 1) * P, :], in_=pv[t // 2][:, t % 2, :])
+
+        xb, db = {}, {}
+
+        def new_xb(s, g):
+            xb[s, g] = group.tile([P, PACK * W_MAX], BF16, name="xb", align_bytes=64)
+
+        def four(dst, src, c0, c1):
+            o = dst[:, PACK * c0 : PACK * c1].rearrange("p (c i t) -> p c t i", i=4, t=PACK)
+            i = src[:, :, c0:c1].rearrange("p t (c i) -> p c t i", i=4)
+            return o, i
+
+        def cast_x(s, g, eng, c0, c1):
+            o, i = four(xb[s, g], xr[s, g], c0, c1)
+            if eng == "v":
+                nc.vector.tensor_copy(out=o, in_=i)
+            else:
+                nc.scalar.copy(out=o, in_=i)
+
+        def quant_x(s, g):
+            w = SLICES[s][1]
+            nc.vector.quantize_mx(out=xq[s, g][:].bitcast(FP8X4), scales=xs[s, g][:], in_=xb[s, g][:, : PACK * w])
+
+        def new_db(g):
+            db[g] = group.tile([P, PACK * R], BF16, name="db", align_bytes=64)
+
+        def cast_d(g, eng, m0, m1):
+            o = db[g][:].rearrange("p (t m j) -> p m j t", t=4, j=PACK)[:, m0:m1]
+            i = dr[g][:].rearrange("p j (m t) -> p m j t", t=4)[:, m0:m1]
+            if eng == "v":
+                nc.vector.tensor_copy(out=o, in_=i)
+            else:
+                nc.scalar.copy(out=o, in_=i)
+
+        def quant_d(g):
+            nc.vector.quantize_mx(out=dq[g][:].bitcast(FP8X4), scales=ds[g][:], in_=db[g][:])
+
+        hp, hf, hb, hq, hs = {}, {}, {}, {}, {}
+
+        def h_mm(s, g):
+            w = SLICES[s][1]
+            for j in range(PACK):
+                if g == 0:
+                    hp[s, j] = psum.tile([P, W_MAX], F32, name=f"h{j}")
+                cols = slice(j * P, (j + 1) * P)
+                nc.tensor.matmul_mx(
+                    out=hp[s, j][:, :w],
+                    lhsT=dq[g][:, cols].bitcast(FP8X4),
+                    lhsT_scale=ds[g][:, cols],
+                    rhs=xq[s, g][:].bitcast(FP8X4),
+                    rhs_scale=xs[s, g][:],
+                    start=(g == 0),
+                    stop=(g == GROUPS - 1),
+                )
+
+        def h_new(s):
+            w = SLICES[s][1]
+            hf[s] = hsb.tile([P, PACK, W_MAX], F32, name="hf")
+            hb[s] = hsb.tile([P, PACK * W_MAX], BF16, name="hb", align_bytes=64)
+            hq[s] = keep.tile([P, w], U32, name=f"hq{s}", align_bytes=64)
+            hs[s] = keep.tile([P, w], U8, name=f"hs{s}", align_bytes=64)
+
+        def h_evac(s, j, eng="s"):
+            w = SLICES[s][1]
+            if eng == "s":
+                nc.scalar.copy(out=hf[s][:, j, :w], in_=hp[s, j][:, :w])
+            else:
+                nc.vector.tensor_copy(out=hf[s][:, j, :w], in_=hp[s, j][:, :w])
+
+        def h_inter(s, eng, c0, c1):
+            o, i = four(hb[s], hf[s], c0, c1)
+            if eng == "v":
+                nc.vector.tensor_copy(out=o, in_=i)
+            else:
+                nc.scalar.copy(out=o, in_=i)
+
+        def h_quant(s):
+            w = SLICES[s][1]
+            nc.vector.quantize_mx(out=hq[s][:].bitcast(FP8X4), scales=hs[s][:], in_=hb[s][:, : PACK * w])
+
+        yp = {}
+
+        def where(t):
+            for s, (t0, w) in enumerate(SLICES):
+                if t0 <= t * P < t0 + w:
+                    return s, t * P - t0
+
+        def y_w(t, n, g):
+            s, c = where(t)
+            cols = slice(c, c + P)
+            n_cols = slice(n * N_TILE, (n + 1) * N_TILE)
+            if g == 0:
+                yp[t, n] = psum.tile([P, N_TILE], F32, name=f"{'y' if t < 6 else 'h'}{(2 * t + n) % 4}")
+            if g < 2:
+                rhs = w8[:, g, n_cols].bitcast(FP8X4)
+            else:
+                rhs = w4[:, g - 2, 2 * n * N_TILE : 2 * (n + 1) * N_TILE].bitcast(FP4X4)
+            nc.tensor.matmul_mx(
+                out=yp[t, n][:],
+                lhsT=xq[s, g][:, cols].bitcast(FP8X4),
+                lhsT_scale=xs[s, g][:, cols],
+                rhs=rhs,
+                rhs_scale=sc[:, g, n_cols],
+                start=(g == 0),
+                stop=False,
+            )
+
+        def y_up(t, n):
+            s, c = where(t)
+            cols = slice(c, c + P)
+            n_cols = slice(n * N_TILE, (n + 1) * N_TILE)
+            nc.tensor.matmul_mx(
+                out=yp[t, n][:],
+                lhsT=hq[s][:, cols].bitcast(FP8X4),
+                lhsT_scale=hs[s][:, cols],
+                rhs=up[:, 2 * n * N_TILE : 2 * (n + 1) * N_TILE].bitcast(FP4X4),
+                rhs_scale=sc[:, 4, n_cols],
+                start=False,
+                stop=True,
+            )
+
+        def y_out(t, n):
+            dst = pv[t // 2][:, t % 2, n * N_TILE : (n + 1) * N_TILE]
+            nc.vector.tensor_tensor(out=dst, in0=yp[t, n][:], in1=dst, op=ADD)
+
+        yf = {}
+
+        def y_evac(t, n):
+            if n == 0:
+                yf[t] = xraw.tile([P, M], F32, name=f"xr0{t}")
+            nc.scalar.copy(out=yf[t][:, n * N_TILE : (n + 1) * N_TILE], in_=yp[t, n][:])
+
+        def y_add(t):
+            dst = pv[t // 2][:, t % 2, :]
+            nc.vector.tensor_tensor(out=dst, in0=yf[t][:], in1=dst, op=ADD)
+
+        def x_split(s, g, cut):
+            w = SLICES[s][1]
+            new_xb(s, g)
+            cast_x(s, g, "s", 0, cut)
+            cast_x(s, g, "v", cut, w)
+
+        def y_w_all(t):
+            for n in (0, 1):
+                for g in range(GROUPS):
+                    y_w(t, n, g)
+
+        nc.vector.memset(sc[:].rearrange("p a n -> p (a n)").bitcast(I32), 0)
+        for g in range(GROUPS):
+            load_x(0, g)
+            load_d(g)
+            if g < 3:
+                load_scales(g)
+        load_w8(0)
+        load_w8(1)
+        load_w4()
+        load_up()
+        for s in (1, 2):
+            for g in range(GROUPS):
+                load_x(s, g)
+        for b in range(4):
+            load_prev(b)
+
+        for g in range(GROUPS):
+            new_xb(0, g)
+            new_db(g)
+            cast_x(0, g, "s", 0, 256)
+            cast_d(g, "s", 0, 48)
+            cast_d(g, "v", 48, 128)
+            quant_x(0, g)
+            quant_d(g)
+            h_mm(0, g)
+        h_new(0)
+        for j in range(PACK):
+            h_evac(0, j)
+        for g in range(GROUPS):
+            for t in (0, 1):
+                for n in (0, 1):
+                    y_w(t, n, g)
+        h_inter(0, "v", 0, 256)
+        h_quant(0)
+        for t in (0, 1):
+            for n in (0, 1):
+                y_up(t, n)
+        x_split(1, 0, 128)
+        x_split(1, 1, 128)
+        quant_x(1, 0)
+        h_mm(1, 0)
+        x_split(1, 2, 128)
+        quant_x(1, 1)
+        h_mm(1, 1)
+        y_evac(0, 0)
+        y_evac(0, 1)
+        x_split(1, 3, 128)
+        quant_x(1, 2)
+        h_mm(1, 2)
+        y_evac(1, 0)
+        y_evac(1, 1)
+        quant_x(1, 3)
+        h_mm(1, 3)
+        h_new(1)
+        for j in range(PACK):
+            h_evac(1, j)
+        y_w_all(2)
+        x_split(2, 0, 192)
+        h_inter(1, "v", 0, 256)
+        quant_x(2, 0)
+        h_quant(1)
+        y_w_all(3)
+        x_split(2, 1, 192)
+        for t in (2, 3):
+            for n in (0, 1):
+                y_up(t, n)
+        h_mm(2, 0)
+        quant_x(2, 1)
+        h_mm(2, 1)
+        x_split(2, 2, 192)
+        y_evac(2, 0)
+        y_evac(2, 1)
+        quant_x(2, 2)
+        y_evac(3, 0)
+        y_evac(3, 1)
+        h_mm(2, 2)
+        new_xb(2, 3)
+        cast_x(2, 3, "v", 128, 512)
+        cast_x(2, 3, "s", 0, 128)
+        for n in (0, 1):
+            for g in range(3):
+                y_w(4, n, g)
+        quant_x(2, 3)
+        h_mm(2, 3)
+        h_new(2)
+        for j in range(PACK):
+            h_evac(2, j)
+        for n in (0, 1):
+            y_w(4, n, 3)
+        y_w_all(5)
+        for t in (0, 1):
+            y_add(t)
+            store(t)
+        h_inter(2, "s", 0, 192)
+        h_inter(2, "v", 192, 512)
+        h_quant(2)
+        for g in range(GROUPS):
+            y_w(6, 0, g)
+        for t in (2, 3):
+            y_add(t)
+            store(t)
+        for t in (4, 5):
+            for n in (0, 1):
+                y_up(t, n)
+        for g in range(GROUPS):
+            y_w(6, 1, g)
+        for n in (0, 1):
+            y_up(6, n)
+        y_w_all(7)
+        for n in (0, 1):
+            y_up(7, n)
+        for t in (4, 5, 6):
+            for n in (0, 1):
+                y_out(t, n)
+            store(t)
+        for n in (0, 1):
+            y_out(7, n)
+        store(7)

@@ -22,6 +22,8 @@ N_TILE = 512
 GROUPS = K // K_PASS
 SLICES = ((0, 256), (256, 256), (512, 512))
 W_MAX = 512
+Y_BANKS = ("a0", "a1"), ("a2", "a3"), ("b0", "b1"), ("a0", "a1"), ("b0", "b1"), ("a0", "a1"), ("a2", "a3"), ("b2", "b3")
+H_BANKS = ("b0", "b1", "b2", "b3"), ("b2", "b2", "b3", "b3"), ("a2", "a3", "b2", "b3")
 
 
 def tile_mix_three_tm_res_kernel(
@@ -74,18 +76,16 @@ def tile_mix_three_tm_res_kernel(
         def load_up():
             nc.sync.dma_start(out=up[:].bitcast(I32), in_=up_words[0].bitcast(I32))
 
-        def load_scales(which):
-            for q in range(4):
-                rows = slice(32 * q, 32 * q + 4)
-                src = slice(4 * q, 4 * q + 4)
+        def load_scales(eng, which):
+            for r in range(4):
                 if which == 2:
-                    nc.sync.dma_start(out=sc[rows, 4, :].bitcast(I32), in_=up_scales[0, src, :].bitcast(I32))
+                    dst = sc[r:P:32, 4, :]
+                    src = up_scales[0].rearrange("(q r) n -> r q n", r=4)[r]
                 else:
                     scales = (w8_scales, w4_scales)[which]
-                    nc.sync.dma_start(
-                        out=sc[rows, 2 * which : 2 * which + 2, :].bitcast(I32),
-                        in_=scales[:, src, :].rearrange("a r n -> r a n").bitcast(I32),
-                    )
+                    dst = sc[r:P:32, 2 * which : 2 * which + 2, :]
+                    src = scales.rearrange("a (q r) n -> r q a n", r=4)[r]
+                eng.dma_start(out=dst.bitcast(I32), in_=src.bitcast(I32))
 
         def load_prev(b):
             rows = prev[b * 256 : (b + 1) * 256, :]
@@ -93,6 +93,10 @@ def tile_mix_three_tm_res_kernel(
 
         def store(t):
             nc.sync.dma_start(out=out[t * P : (t + 1) * P, :], in_=pv[t // 2][:, t % 2, :])
+
+        def store_half(t, n):
+            n_cols = slice(n * N_TILE, (n + 1) * N_TILE)
+            nc.sync.dma_start(out=out[t * P : (t + 1) * P, n_cols], in_=pv[t // 2][:, t % 2, n_cols])
 
         xb, db = {}, {}
 
@@ -131,35 +135,42 @@ def tile_mix_three_tm_res_kernel(
 
         hp, hf, hb, hq, hs = {}, {}, {}, {}, {}
 
-        def h_mm(s, g):
+        def h_mm(s, j, g):
             w = SLICES[s][1]
-            for j in range(PACK):
-                if g == 0:
-                    hp[s, j] = psum.tile([P, W_MAX], F32, name=f"h{j}")
-                cols = slice(j * P, (j + 1) * P)
-                nc.tensor.matmul_mx(
-                    out=hp[s, j][:, :w],
-                    lhsT=dq[g][:, cols].bitcast(FP8X4),
-                    lhsT_scale=ds[g][:, cols],
-                    rhs=xq[s, g][:].bitcast(FP8X4),
-                    rhs_scale=xs[s, g][:],
-                    start=(g == 0),
-                    stop=(g == GROUPS - 1),
-                )
+            shared = s == 1
+            if g == 0 and not (shared and j % 2):
+                hp[s, j] = psum.tile([P, W_MAX], F32, name=H_BANKS[s][j])
+                if shared:
+                    hp[s, j + 1] = hp[s, j]
+            c0 = w * (j % 2) if shared else 0
+            cols = slice(j * P, (j + 1) * P)
+            nc.tensor.matmul_mx(
+                out=hp[s, j][:, c0 : c0 + w],
+                lhsT=dq[g][:, cols].bitcast(FP8X4),
+                lhsT_scale=ds[g][:, cols],
+                rhs=xq[s, g][:].bitcast(FP8X4),
+                rhs_scale=xs[s, g][:],
+                start=(g == 0),
+                stop=(g == GROUPS - 1),
+            )
 
         def h_new(s):
             w = SLICES[s][1]
-            hf[s] = hsb.tile([P, PACK, W_MAX], F32, name="hf")
+            hf[s] = hsb.tile([P, PACK, w], F32, name="hf")
             hb[s] = hsb.tile([P, PACK * W_MAX], BF16, name="hb", align_bytes=64)
             hq[s] = keep.tile([P, w], U32, name=f"hq{s}", align_bytes=64)
             hs[s] = keep.tile([P, w], U8, name=f"hs{s}", align_bytes=64)
 
         def h_evac(s, j, eng="s"):
             w = SLICES[s][1]
-            if eng == "s":
-                nc.scalar.copy(out=hf[s][:, j, :w], in_=hp[s, j][:, :w])
+            if s == 1:
+                dst, src = hf[s][:, j : j + 2, :].rearrange("p j w -> p (j w)"), hp[s, j][:]
             else:
-                nc.vector.tensor_copy(out=hf[s][:, j, :w], in_=hp[s, j][:, :w])
+                dst, src = hf[s][:, j, :], hp[s, j][:, :w]
+            if eng == "s":
+                nc.scalar.copy(out=dst, in_=src)
+            else:
+                nc.vector.tensor_copy(out=dst, in_=src)
 
         def h_inter(s, eng, c0, c1):
             o, i = four(hb[s], hf[s], c0, c1)
@@ -184,7 +195,7 @@ def tile_mix_three_tm_res_kernel(
             cols = slice(c, c + P)
             n_cols = slice(n * N_TILE, (n + 1) * N_TILE)
             if g == 0:
-                yp[t, n] = psum.tile([P, N_TILE], F32, name=f"{'y' if t < 6 else 'h'}{(2 * t + n) % 4}")
+                yp[t, n] = psum.tile([P, N_TILE], F32, name=Y_BANKS[t][n])
             if g < 2:
                 rhs = w8[:, g, n_cols].bitcast(FP8X4)
             else:
@@ -240,33 +251,46 @@ def tile_mix_three_tm_res_kernel(
                     y_w(t, n, g)
 
         nc.vector.memset(sc[:].rearrange("p a n -> p (a n)").bitcast(I32), 0)
+        load_scales(nc.gpsimd, 1)
+        for g in range(GROUPS):
+            load_d(g)
+            if g < 2:
+                load_scales(nc.sync, 2 * g)
         for g in range(GROUPS):
             load_x(0, g)
-            load_d(g)
-            if g < 3:
-                load_scales(g)
         load_w8(0)
         load_w8(1)
         load_w4()
+        load_x(1, 0)
+        load_x(1, 1)
         load_up()
-        for s in (1, 2):
-            for g in range(GROUPS):
-                load_x(s, g)
+        load_x(1, 2)
+        load_x(1, 3)
+        for g in range(GROUPS):
+            load_x(2, g)
         for b in range(4):
             load_prev(b)
 
         for g in range(GROUPS):
-            new_xb(0, g)
             new_db(g)
-            cast_x(0, g, "s", 0, 256)
             cast_d(g, "s", 0, 48)
             cast_d(g, "v", 48, 128)
-            quant_x(0, g)
-            quant_d(g)
-            h_mm(0, g)
+            if g:
+                quant_d(g - 1)
+        for g in range(GROUPS):
+            x_split(0, g, 128)
+            if g == 0:
+                quant_d(3)
+            else:
+                quant_x(0, g - 1)
+                for j in range(PACK):
+                    h_mm(0, j, g - 1)
+        quant_x(0, 3)
+        for j in range(PACK):
+            h_mm(0, j, 3)
         h_new(0)
         for j in range(PACK):
-            h_evac(0, j)
+            h_evac(0, j, "svsv"[j])
         for g in range(GROUPS):
             for t in (0, 1):
                 for n in (0, 1):
@@ -276,53 +300,58 @@ def tile_mix_three_tm_res_kernel(
         for t in (0, 1):
             for n in (0, 1):
                 y_up(t, n)
-        x_split(1, 0, 128)
-        x_split(1, 1, 128)
-        quant_x(1, 0)
-        h_mm(1, 0)
-        x_split(1, 2, 128)
-        quant_x(1, 1)
-        h_mm(1, 1)
-        y_evac(0, 0)
-        y_evac(0, 1)
-        x_split(1, 3, 128)
-        quant_x(1, 2)
-        h_mm(1, 2)
-        y_evac(1, 0)
+        for g in range(GROUPS):
+            x_split(1, g, 128)
+            if g == 1:
+                y_evac(0, 0)
+                y_evac(0, 1)
+            if g == 2:
+                y_evac(1, 0)
+            if g:
+                quant_x(1, g - 1)
         y_evac(1, 1)
         quant_x(1, 3)
-        h_mm(1, 3)
-        h_new(1)
+        for t in (2, 3):
+            for g in range(3):
+                for n in (0, 1):
+                    y_w(t, n, g)
         for j in range(PACK):
-            h_evac(1, j)
-        y_w_all(2)
+            for g in range(GROUPS):
+                h_mm(1, j, g)
+        for t in (2, 3):
+            for n in (0, 1):
+                y_w(t, n, 3)
+        h_new(1)
         x_split(2, 0, 192)
-        h_inter(1, "v", 0, 256)
+        h_evac(1, 0, "s")
         quant_x(2, 0)
-        h_quant(1)
-        y_w_all(3)
         x_split(2, 1, 192)
+        h_evac(1, 2, "v")
+        h_inter(1, "v", 0, 256)
+        h_quant(1)
+        for j in range(PACK):
+            h_mm(2, j, 0)
         for t in (2, 3):
             for n in (0, 1):
                 y_up(t, n)
-        h_mm(2, 0)
-        quant_x(2, 1)
-        h_mm(2, 1)
         x_split(2, 2, 192)
         y_evac(2, 0)
         y_evac(2, 1)
-        quant_x(2, 2)
+        quant_x(2, 1)
+        for j in range(PACK):
+            h_mm(2, j, 1)
         y_evac(3, 0)
         y_evac(3, 1)
-        h_mm(2, 2)
-        new_xb(2, 3)
-        cast_x(2, 3, "v", 128, 512)
-        cast_x(2, 3, "s", 0, 128)
+        quant_x(2, 2)
+        for j in range(PACK):
+            h_mm(2, j, 2)
+        x_split(2, 3, 192)
         for n in (0, 1):
             for g in range(3):
                 y_w(4, n, g)
         quant_x(2, 3)
-        h_mm(2, 3)
+        for j in range(PACK):
+            h_mm(2, j, 3)
         h_new(2)
         for j in range(PACK):
             h_evac(2, j)
@@ -343,17 +372,17 @@ def tile_mix_three_tm_res_kernel(
         for t in (4, 5):
             for n in (0, 1):
                 y_up(t, n)
+                y_out(t, n)
+            store(t)
         for g in range(GROUPS):
             y_w(6, 1, g)
         for n in (0, 1):
             y_up(6, n)
-        y_w_all(7)
+            y_out(6, n)
+        store(6)
         for n in (0, 1):
+            for g in range(GROUPS):
+                y_w(7, n, g)
             y_up(7, n)
-        for t in (4, 5, 6):
-            for n in (0, 1):
-                y_out(t, n)
-            store(t)
-        for n in (0, 1):
             y_out(7, n)
-        store(7)
+            store_half(7, n)

@@ -76,16 +76,15 @@ def tile_mix_three_tm_res_kernel(
         def load_up():
             nc.sync.dma_start(out=up[:].bitcast(I32), in_=up_words[0].bitcast(I32))
 
-        def load_scales(eng, which):
-            for r in range(4):
-                if which == 2:
-                    dst = sc[r:P:32, 4, :]
-                    src = up_scales[0].rearrange("(q r) n -> r q n", r=4)[r]
-                else:
-                    scales = (w8_scales, w4_scales)[which]
-                    dst = sc[r:P:32, 2 * which : 2 * which + 2, :]
-                    src = scales.rearrange("a (q r) n -> r q a n", r=4)[r]
-                eng.dma_start(out=dst.bitcast(I32), in_=src.bitcast(I32))
+        def load_scales(which, r):
+            if which == 2:
+                dst = sc[r:P:32, 4, :]
+                src = up_scales[0].rearrange("(q r) n -> r q n", r=4)[r]
+            else:
+                scales = (w8_scales, w4_scales)[which]
+                dst = sc[r:P:32, 2 * which : 2 * which + 2, :]
+                src = scales.rearrange("a (q r) n -> r q a n", r=4)[r]
+            nc.sync.dma_start(out=dst.bitcast(I32), in_=src.bitcast(I32))
 
         def load_prev(b):
             rows = prev[b * 256 : (b + 1) * 256, :]
@@ -123,12 +122,13 @@ def tile_mix_three_tm_res_kernel(
             db[g] = group.tile([P, PACK * R], BF16, name="db", align_bytes=64)
 
         def cast_d(g, eng, m0, m1):
-            o = db[g][:].rearrange("p (t m j) -> p m j t", t=4, j=PACK)[:, m0:m1]
-            i = dr[g][:].rearrange("p j (m t) -> p m j t", t=4)[:, m0:m1]
-            if eng == "v":
-                nc.vector.tensor_copy(out=o, in_=i)
-            else:
-                nc.scalar.copy(out=o, in_=i)
+            for t in (0, 2):
+                o = db[g][:].rearrange("p (t m j) -> p m j t", t=4, j=PACK)[:, m0:m1, :, t : t + 2]
+                i = dr[g][:].rearrange("p j (m t) -> p m j t", t=4)[:, m0:m1, :, t : t + 2]
+                if eng == "v":
+                    nc.vector.tensor_copy(out=o, in_=i)
+                else:
+                    nc.scalar.copy(out=o, in_=i)
 
         def quant_d(g):
             nc.vector.quantize_mx(out=dq[g][:].bitcast(FP8X4), scales=ds[g][:], in_=db[g][:])
@@ -251,13 +251,14 @@ def tile_mix_three_tm_res_kernel(
                     y_w(t, n, g)
 
         nc.vector.memset(sc[:].rearrange("p a n -> p (a n)").bitcast(I32), 0)
-        load_scales(nc.gpsimd, 1)
+        scale_loads = [(which, r) for which in range(3) for r in range(4)]
         for g in range(GROUPS):
             load_d(g)
-            if g < 2:
-                load_scales(nc.sync, 2 * g)
+            load_scales(*scale_loads[2 * g])
+            load_scales(*scale_loads[2 * g + 1])
         for g in range(GROUPS):
             load_x(0, g)
+            load_scales(*scale_loads[8 + g])
         load_w8(0)
         load_w8(1)
         load_w4()
@@ -358,7 +359,7 @@ def tile_mix_three_tm_res_kernel(
         for n in (0, 1):
             y_w(4, n, 3)
         y_w_all(5)
-        for t in (0, 1):
+        for t in (0, 1, 2):
             y_add(t)
             store(t)
         h_inter(2, "s", 0, 192)
@@ -366,9 +367,8 @@ def tile_mix_three_tm_res_kernel(
         h_quant(2)
         for g in range(GROUPS):
             y_w(6, 0, g)
-        for t in (2, 3):
-            y_add(t)
-            store(t)
+        y_add(3)
+        store(3)
         for t in (4, 5):
             for n in (0, 1):
                 y_up(t, n)

@@ -103,8 +103,8 @@ def tile_mix_three_tm_res_kernel(
             xb[s, g] = group.tile([P, PACK * W_MAX], BF16, name="xb", align_bytes=64)
 
         def four(dst, src, c0, c1):
-            o = dst[:, PACK * c0 : PACK * c1].rearrange("p (c i t) -> p c t i", i=4, t=PACK)
-            i = src[:, :, c0:c1].rearrange("p t (c i) -> p c t i", i=4)
+            o = dst[:, PACK * c0 : PACK * c1].rearrange("p (c j) -> p c j", j=PACK)
+            i = src[:, :, c0:c1].rearrange("p j c -> p c j")
             return o, i
 
         def cast_x(s, g, eng, c0, c1):
@@ -116,19 +116,24 @@ def tile_mix_three_tm_res_kernel(
 
         def quant_x(s, g):
             w = SLICES[s][1]
-            nc.vector.quantize_mx(out=xq[s, g][:].bitcast(FP8X4), scales=xs[s, g][:], in_=xb[s, g][:, : PACK * w])
+            parts = ((0, 128), (128, 256)) if w == 256 else ((0, w),)
+            for c0, c1 in parts:
+                nc.vector.quantize_mx(
+                    out=xq[s, g][:, c0:c1].bitcast(FP8X4),
+                    scales=xs[s, g][:, c0:c1],
+                    in_=xb[s, g][:, PACK * c0 : PACK * c1],
+                )
 
         def new_db(g):
             db[g] = group.tile([P, PACK * R], BF16, name="db", align_bytes=64)
 
         def cast_d(g, eng, m0, m1):
-            for t in (0, 2):
-                o = db[g][:].rearrange("p (t m j) -> p m j t", t=4, j=PACK)[:, m0:m1, :, t : t + 2]
-                i = dr[g][:].rearrange("p j (m t) -> p m j t", t=4)[:, m0:m1, :, t : t + 2]
-                if eng == "v":
-                    nc.vector.tensor_copy(out=o, in_=i)
-                else:
-                    nc.scalar.copy(out=o, in_=i)
+            o = db[g][:].rearrange("p (t m j) -> p m t j", t=4, j=PACK)[:, m0:m1]
+            i = dr[g][:].rearrange("p j (m t) -> p m t j", t=4)[:, m0:m1]
+            if eng == "v":
+                nc.vector.tensor_copy(out=o, in_=i)
+            else:
+                nc.scalar.copy(out=o, in_=i)
 
         def quant_d(g):
             nc.vector.quantize_mx(out=dq[g][:].bitcast(FP8X4), scales=ds[g][:], in_=db[g][:])
@@ -230,10 +235,14 @@ def tile_mix_three_tm_res_kernel(
 
         yf = {}
 
-        def y_evac(t, n):
+        def y_evac(t, n, eng="s"):
             if n == 0:
                 yf[t] = xraw.tile([P, M], F32, name=f"xr0{t}")
-            nc.scalar.copy(out=yf[t][:, n * N_TILE : (n + 1) * N_TILE], in_=yp[t, n][:])
+            dst = yf[t][:, n * N_TILE : (n + 1) * N_TILE]
+            if eng == "s":
+                nc.scalar.copy(out=dst, in_=yp[t, n][:])
+            else:
+                nc.vector.tensor_copy(out=dst, in_=yp[t, n][:])
 
         def y_add(t):
             dst = pv[t // 2][:, t % 2, :]
@@ -274,21 +283,17 @@ def tile_mix_three_tm_res_kernel(
 
         for g in range(GROUPS):
             new_db(g)
-            cast_d(g, "s", 0, 48)
-            cast_d(g, "v", 48, 128)
+            cast_d(g, "s", 0, 64)
+            cast_d(g, "v", 64, 128)
             if g:
                 quant_d(g - 1)
         for g in range(GROUPS):
             x_split(0, g, 128)
+            quant_x(0, g)
             if g == 0:
                 quant_d(3)
-            else:
-                quant_x(0, g - 1)
-                for j in range(PACK):
-                    h_mm(0, j, g - 1)
-        quant_x(0, 3)
-        for j in range(PACK):
-            h_mm(0, j, 3)
+            for j in range(PACK):
+                h_mm(0, j, g)
         h_new(0)
         for j in range(PACK):
             h_evac(0, j, "svsv"[j])
@@ -297,21 +302,21 @@ def tile_mix_three_tm_res_kernel(
                 for n in (0, 1):
                     y_w(t, n, g)
         h_inter(0, "v", 0, 256)
+        x_split(1, 0, 128)
         h_quant(0)
+        x_split(1, 1, 128)
+        quant_x(1, 0)
+        quant_x(1, 1)
         for t in (0, 1):
             for n in (0, 1):
                 y_up(t, n)
-        for g in range(GROUPS):
-            x_split(1, g, 128)
-            if g == 1:
-                y_evac(0, 0)
-                y_evac(0, 1)
-            if g == 2:
-                y_evac(1, 0)
-            if g:
-                quant_x(1, g - 1)
-        y_evac(1, 1)
+        x_split(1, 2, 128)
+        quant_x(1, 2)
+        y_evac(0, 0)
+        y_evac(0, 1)
+        x_split(1, 3, 128)
         quant_x(1, 3)
+        y_evac(1, 0, "v")
         for t in (2, 3):
             for g in range(3):
                 for n in (0, 1):
@@ -324,29 +329,30 @@ def tile_mix_three_tm_res_kernel(
                 y_w(t, n, 3)
         h_new(1)
         x_split(2, 0, 192)
-        h_evac(1, 0, "s")
+        y_evac(1, 1, "v")
         quant_x(2, 0)
         x_split(2, 1, 192)
-        h_evac(1, 2, "v")
+        h_evac(1, 0, "s")
+        h_evac(1, 2, "s")
+        quant_x(2, 1)
         h_inter(1, "v", 0, 256)
         h_quant(1)
         for j in range(PACK):
             h_mm(2, j, 0)
+        for j in range(PACK):
+            h_mm(2, j, 1)
         for t in (2, 3):
             for n in (0, 1):
                 y_up(t, n)
-        x_split(2, 2, 192)
+        x_split(2, 2, 288)
         y_evac(2, 0)
         y_evac(2, 1)
-        quant_x(2, 1)
-        for j in range(PACK):
-            h_mm(2, j, 1)
-        y_evac(3, 0)
-        y_evac(3, 1)
         quant_x(2, 2)
         for j in range(PACK):
             h_mm(2, j, 2)
         x_split(2, 3, 192)
+        y_evac(3, 0)
+        y_evac(3, 1)
         for n in (0, 1):
             for g in range(3):
                 y_w(4, n, g)

from contextlib import ExitStack

import concourse.mybir as mybir

O, K, R, M, T = 1024, 2048, 512, 1024, 1024
FLOPS = 2 * T * (K * R + K * M + R * M)
BYTES = 4 * (K * T + K * R + 2 * T * M) + O * M + (K - O) * M // 2 + R * M // 2 + (K + R) * M // 32

F32 = mybir.dt.float32
BF16 = mybir.dt.bfloat16
U32 = mybir.dt.uint32
I32 = mybir.dt.int32
U8 = mybir.dt.uint8
FP8X4 = mybir.dt.float8_e4m3fn_x4
FP4X4 = mybir.dt.float4_e2m1fn_x4
ADD = mybir.AluOpType.add

P = 128
PACK = 4
K_PASS = P * PACK
N_TILE = 512
GROUPS = K // K_PASS
SLICES = ((0, 256), (256, 256), (512, 512))
W_MAX = 512
Y_BANKS = ("a0", "a1"), ("a2", "a3"), ("b0", "b1"), ("a0", "a1"), ("b0", "b1"), ("a0", "a1"), ("a2", "a3"), ("b2", "b3")
H_BANKS = ("b0", "b1", "b2", "b3"), ("b2", "b2", "b3", "b3"), ("a2", "a3", "b2", "b3")


def tile_mix_three_tm_res_kernel(
    tc, x, w8_words, w8_scales, w4_words, w4_scales, down, up_words, up_scales, prev, out
):
    nc = tc.nc
    with ExitStack() as ctx:
        keep = ctx.enter_context(tc.tile_pool(name="keep", bufs=1))
        xraw = ctx.enter_context(tc.tile_pool(name="xraw", bufs=1))
        draw = ctx.enter_context(tc.tile_pool(name="draw", bufs=4))
        group = ctx.enter_context(tc.tile_pool(name="group", bufs=3))
        hsb = ctx.enter_context(tc.tile_pool(name="hsb", bufs=1))
        psum = ctx.enter_context(tc.psum_pool(name="psum", bufs=1))
        ctx.enter_context(tc.manual_schedule())

        w8 = keep.tile([P, 2, M], U32, name="w8", align_bytes=64)
        w4 = keep.tile([P, 2, 2 * M], U8, name="w4", align_bytes=64)
        up = keep.tile([P, 2 * M], U8, name="up", align_bytes=64)
        sc = keep.tile([P, 5, M], U8, name="sc", align_bytes=64)
        xq, xs, xr = {}, {}, {}
        dq, ds, dr = {}, {}, {}
        for s, (t0, w) in enumerate(SLICES):
            for g in range(GROUPS):
                xq[s, g] = keep.tile([P, w], U32, name=f"xq{s}{g}", align_bytes=64)
                xs[s, g] = keep.tile([P, w], U8, name=f"xs{s}{g}", align_bytes=64)
        for g in range(GROUPS):
            dq[g] = keep.tile([P, R], U32, name=f"dq{g}", align_bytes=64)
            ds[g] = keep.tile([P, R], U8, name=f"ds{g}", align_bytes=64)
        pv = [keep.tile([P, 2, M], F32, name=f"pv{b}") for b in range(4)]

        def load_x(s, g):
            t0, w = SLICES[s]
            xr[s, g] = xraw.tile([P, PACK, w], F32, name=f"xr{s}{g}")
            rows = x[g * K_PASS : (g + 1) * K_PASS, t0 : t0 + w]
            nc.sync.dma_start(out=xr[s, g][:], in_=rows.rearrange("(p j) w -> p j w", j=PACK))

        def load_d(g):
            dr[g] = draw.tile([P, PACK, R], F32, name="dr")
            rows = down[g * K_PASS : (g + 1) * K_PASS, :]
            nc.sync.dma_start(out=dr[g][:], in_=rows.rearrange("(p j) r -> p j r", j=PACK))

        def load_w8(a):
            nc.sync.dma_start(
                out=w8[:, a, :].bitcast(I32), in_=w8_words[a].rearrange("p n i -> p (n i)").bitcast(I32)
            )

        def load_w4():
            nc.sync.dma_start(out=w4[:].bitcast(I32), in_=w4_words.rearrange("a p n -> p a n").bitcast(I32))

        def load_up():
            nc.sync.dma_start(out=up[:].bitcast(I32), in_=up_words[0].bitcast(I32))

        def load_scales(which, r):
            if which == 2:
                dst = sc[r:P:32, 4, :]
                src = up_scales[0].rearrange("(q r) n -> r q n", r=4)[r]
            else:
                scales = (w8_scales, w4_scales)[which]
                dst = sc[r:P:32, 2 * which : 2 * which + 2, :]
                src = scales.rearrange("a (q r) n -> r q a n", r=4)[r]
            nc.sync.dma_start(out=dst.bitcast(I32), in_=src.bitcast(I32))

        def load_prev(b):
            rows = prev[b * 256 : (b + 1) * 256, :]
            nc.sync.dma_start(out=pv[b][:], in_=rows.rearrange("(a p) n -> p a n", p=P))

        def store(t):
            nc.sync.dma_start(out=out[t * P : (t + 1) * P, :], in_=pv[t // 2][:, t % 2, :])

        def store_half(t, n):
            n_cols = slice(n * N_TILE, (n + 1) * N_TILE)
            nc.sync.dma_start(out=out[t * P : (t + 1) * P, n_cols], in_=pv[t // 2][:, t % 2, n_cols])

        xb, db = {}, {}

        def new_xb(s, g):
            xb[s, g] = group.tile([P, PACK * W_MAX], BF16, name="xb", align_bytes=64)

        def four(dst, src, c0, c1):
            o = dst[:, PACK * c0 : PACK * c1].rearrange("p (c j) -> p c j", j=PACK)
            i = src[:, :, c0:c1].rearrange("p j c -> p c j")
            return o, i

        def cast_x(s, g, eng, c0, c1):
            o, i = four(xb[s, g], xr[s, g], c0, c1)
            if eng == "v":
                nc.vector.tensor_copy(out=o, in_=i)
            else:
                nc.scalar.copy(out=o, in_=i)

        def quant_x(s, g):
            w = SLICES[s][1]
            parts = ((0, 128), (128, 256)) if w == 256 else ((0, w),)
            for c0, c1 in parts:
                nc.vector.quantize_mx(
                    out=xq[s, g][:, c0:c1].bitcast(FP8X4),
                    scales=xs[s, g][:, c0:c1],
                    in_=xb[s, g][:, PACK * c0 : PACK * c1],
                )

        def new_db(g):
            db[g] = group.tile([P, PACK * R], BF16, name="db", align_bytes=64)

        def cast_d(g, eng, m0, m1):
            o = db[g][:].rearrange("p (t m j) -> p m t j", t=4, j=PACK)[:, m0:m1]
            i = dr[g][:].rearrange("p j (m t) -> p m t j", t=4)[:, m0:m1]
            if eng == "v":
                nc.vector.tensor_copy(out=o, in_=i)
            else:
                nc.scalar.copy(out=o, in_=i)

        def quant_d(g):
            nc.vector.quantize_mx(out=dq[g][:].bitcast(FP8X4), scales=ds[g][:], in_=db[g][:])

        hp, hf, hb, hq, hs = {}, {}, {}, {}, {}

        def h_mm(s, j, g):
            w = SLICES[s][1]
            shared = s == 1
            if g == 0 and not (shared and j % 2):
                hp[s, j] = psum.tile([P, W_MAX], F32, name=H_BANKS[s][j])
                if shared:
                    hp[s, j + 1] = hp[s, j]
            c0 = w * (j % 2) if shared else 0
            cols = slice(j * P, (j + 1) * P)
            nc.tensor.matmul_mx(
                out=hp[s, j][:, c0 : c0 + w],
                lhsT=dq[g][:, cols].bitcast(FP8X4),
                lhsT_scale=ds[g][:, cols],
                rhs=xq[s, g][:].bitcast(FP8X4),
                rhs_scale=xs[s, g][:],
                start=(g == 0),
                stop=(g == GROUPS - 1),
            )

        def h_new(s):
            w = SLICES[s][1]
            hf[s] = hsb.tile([P, PACK, w], F32, name="hf")
            hb[s] = hsb.tile([P, PACK * W_MAX], BF16, name="hb", align_bytes=64)
            hq[s] = keep.tile([P, w], U32, name=f"hq{s}", align_bytes=64)
            hs[s] = keep.tile([P, w], U8, name=f"hs{s}", align_bytes=64)

        def h_evac(s, j, eng="s"):
            w = SLICES[s][1]
            if s == 1:
                dst, src = hf[s][:, j : j + 2, :].rearrange("p j w -> p (j w)"), hp[s, j][:]
            else:
                dst, src = hf[s][:, j, :], hp[s, j][:, :w]
            if eng == "s":
                nc.scalar.copy(out=dst, in_=src)
            else:
                nc.vector.tensor_copy(out=dst, in_=src)

        def h_inter(s, eng, c0, c1):
            o, i = four(hb[s], hf[s], c0, c1)
            if eng == "v":
                nc.vector.tensor_copy(out=o, in_=i)
            else:
                nc.scalar.copy(out=o, in_=i)

        def h_quant(s):
            w = SLICES[s][1]
            nc.vector.quantize_mx(out=hq[s][:].bitcast(FP8X4), scales=hs[s][:], in_=hb[s][:, : PACK * w])

        yp = {}

        def where(t):
            for s, (t0, w) in enumerate(SLICES):
                if t0 <= t * P < t0 + w:
                    return s, t * P - t0

        def y_w(t, n, g):
            s, c = where(t)
            cols = slice(c, c + P)
            n_cols = slice(n * N_TILE, (n + 1) * N_TILE)
            if g == 0:
                yp[t, n] = psum.tile([P, N_TILE], F32, name=Y_BANKS[t][n])
            if g < 2:
                rhs = w8[:, g, n_cols].bitcast(FP8X4)
            else:
                rhs = w4[:, g - 2, 2 * n * N_TILE : 2 * (n + 1) * N_TILE].bitcast(FP4X4)
            nc.tensor.matmul_mx(
                out=yp[t, n][:],
                lhsT=xq[s, g][:, cols].bitcast(FP8X4),
                lhsT_scale=xs[s, g][:, cols],
                rhs=rhs,
                rhs_scale=sc[:, g, n_cols],
                start=(g == 0),
                stop=False,
            )

        def y_up(t, n):
            s, c = where(t)
            cols = slice(c, c + P)
            n_cols = slice(n * N_TILE, (n + 1) * N_TILE)
            nc.tensor.matmul_mx(
                out=yp[t, n][:],
                lhsT=hq[s][:, cols].bitcast(FP8X4),
                lhsT_scale=hs[s][:, cols],
                rhs=up[:, 2 * n * N_TILE : 2 * (n + 1) * N_TILE].bitcast(FP4X4),
                rhs_scale=sc[:, 4, n_cols],
                start=False,
                stop=True,
            )

        def y_out(t, n):
            dst = pv[t // 2][:, t % 2, n * N_TILE : (n + 1) * N_TILE]
            nc.vector.tensor_tensor(out=dst, in0=yp[t, n][:], in1=dst, op=ADD)

        yf = {}

        def y_evac(t, n, eng="s"):
            if n == 0:
                yf[t] = xraw.tile([P, M], F32, name=f"xr0{t}")
            dst = yf[t][:, n * N_TILE : (n + 1) * N_TILE]
            if eng == "s":
                nc.scalar.copy(out=dst, in_=yp[t, n][:])
            else:
                nc.vector.tensor_copy(out=dst, in_=yp[t, n][:])

        def y_add(t):
            dst = pv[t // 2][:, t % 2, :]
            nc.vector.tensor_tensor(out=dst, in0=yf[t][:], in1=dst, op=ADD)

        def x_split(s, g, cut):
            w = SLICES[s][1]
            new_xb(s, g)
            cast_x(s, g, "s", 0, cut)
            cast_x(s, g, "v", cut, w)

        def y_w_all(t):
            for n in (0, 1):
                for g in range(GROUPS):
                    y_w(t, n, g)

        nc.vector.memset(sc[:].rearrange("p a n -> p (a n)").bitcast(I32), 0)
        scale_loads = [(which, r) for which in range(3) for r in range(4)]
        for g in range(GROUPS):
            load_d(g)
            load_scales(*scale_loads[2 * g])
            load_scales(*scale_loads[2 * g + 1])
        for g in range(GROUPS):
            load_x(0, g)
            load_scales(*scale_loads[8 + g])
        load_w8(0)
        load_w8(1)
        load_w4()
        load_x(1, 0)
        load_x(1, 1)
        load_up()
        load_x(1, 2)
        load_x(1, 3)
        for g in range(GROUPS):
            load_x(2, g)
        for b in range(4):
            load_prev(b)

        for g in range(GROUPS):
            new_db(g)
            cast_d(g, "s", 0, 64)
            cast_d(g, "v", 64, 128)
            if g:
                quant_d(g - 1)
        for g in range(GROUPS):
            x_split(0, g, 128)
            quant_x(0, g)
            if g == 0:
                quant_d(3)
            for j in range(PACK):
                h_mm(0, j, g)
        h_new(0)
        for j in range(PACK):
            h_evac(0, j, "svsv"[j])
        for g in range(GROUPS):
            for t in (0, 1):
                for n in (0, 1):
                    y_w(t, n, g)
        h_inter(0, "v", 0, 256)
        x_split(1, 0, 128)
        h_quant(0)
        x_split(1, 1, 128)
        quant_x(1, 0)
        quant_x(1, 1)
        for t in (0, 1):
            for n in (0, 1):
                y_up(t, n)
        x_split(1, 2, 128)
        quant_x(1, 2)
        y_evac(0, 0)
        y_evac(0, 1)
        x_split(1, 3, 128)
        quant_x(1, 3)
        y_evac(1, 0, "v")
        for t in (2, 3):
            for g in range(3):
                for n in (0, 1):
                    y_w(t, n, g)
        for j in range(PACK):
            for g in range(GROUPS):
                h_mm(1, j, g)
        for t in (2, 3):
            for n in (0, 1):
                y_w(t, n, 3)
        h_new(1)
        x_split(2, 0, 192)
        y_evac(1, 1, "v")
        quant_x(2, 0)
        x_split(2, 1, 192)
        h_evac(1, 0, "s")
        h_evac(1, 2, "s")
        quant_x(2, 1)
        h_inter(1, "v", 0, 256)
        h_quant(1)
        for j in range(PACK):
            h_mm(2, j, 0)
        for j in range(PACK):
            h_mm(2, j, 1)
        for t in (2, 3):
            for n in (0, 1):
                y_up(t, n)
        x_split(2, 2, 288)
        y_evac(2, 0)
        y_evac(2, 1)
        quant_x(2, 2)
        for j in range(PACK):
            h_mm(2, j, 2)
        x_split(2, 3, 192)
        y_evac(3, 0)
        y_evac(3, 1)
        for n in (0, 1):
            for g in range(3):
                y_w(4, n, g)
        quant_x(2, 3)
        for j in range(PACK):
            h_mm(2, j, 3)
        h_new(2)
        for j in range(PACK):
            h_evac(2, j)
        for n in (0, 1):
            y_w(4, n, 3)
        y_w_all(5)
        for t in (0, 1, 2):
            y_add(t)
            store(t)
        h_inter(2, "s", 0, 192)
        h_inter(2, "v", 192, 512)
        h_quant(2)
        for g in range(GROUPS):
            y_w(6, 0, g)
        y_add(3)
        store(3)
        for t in (4, 5):
            for n in (0, 1):
                y_up(t, n)
                y_out(t, n)
            store(t)
        for g in range(GROUPS):
            y_w(6, 1, g)
        for n in (0, 1):
            y_up(6, n)
            y_out(6, n)
        store(6)
        for n in (0, 1):
            for g in range(GROUPS):
                y_w(7, n, g)
            y_up(7, n)
            y_out(7, n)
            store_half(7, n)
